import numpy as np
import ml_dtypes


def mxq(x, axis, fmt="e4m3"):
    dtype, down = {"e4m3": (ml_dtypes.float8_e4m3fn, 7), "e5m2": (ml_dtypes.float8_e5m2, 14)}[fmt]
    v = np.moveaxis(np.asarray(x, np.float32).astype(ml_dtypes.bfloat16).astype(np.float64), axis, -1)
    blocks = v.reshape(v.shape[:-1] + (-1, 32))
    amax = np.abs(blocks).max(-1, keepdims=True)
    byte = np.maximum(np.where(amax > 0, np.frexp(amax)[1] - 1 + 127, 0) - down, 1)
    scale = np.exp2(byte - 127.0)
    codes = (blocks / scale).astype(np.float32).astype(dtype).astype(np.float64)
    return np.moveaxis((codes * scale).reshape(v.shape), -1, axis)


WIDE = False


def mx_kscale(k):
    if not WIDE:
        return np.ones(k)
    levels = np.array([10, -10, 5, -5, 0])
    if k % 512:
        return np.exp2(np.random.permutation(np.resize(levels, k // 32))).repeat(32)
    a = np.empty((k // 512, 16))
    for p in range(k // 512):
        a[p, :8] = np.random.permutation(np.resize(levels, 8))
        for g in range(8):
            far = levels[np.abs(levels - a[p, g]) >= 10]
            a[p, g + 8] = far[np.random.randint(len(far))]
    return np.exp2(a.ravel()).repeat(32)


def f64(x):
    return np.asarray(x).astype(np.float64)


def striped(idx):
    return np.tile(np.asarray(idx).reshape(-1, 16).T, (8, 1)).astype(np.uint16)


def unstriped(offs):
    return offs[:16].T.reshape(-1).astype(np.int64)


E2M1 = np.array([0.0, 0.5, 1.0, 1.5, 2.0, 3.0, 4.0, 6.0, -0.0, -0.5, -1.0, -1.5, -2.0, -3.0, -4.0, -6.0])


def pack_weight(w, fmt):
    k, n = w.shape
    w = f64(np.asarray(w, np.float32).astype(ml_dtypes.bfloat16)).reshape(k // 32, 32, n)
    amax = np.abs(w).max(1)
    if fmt == "e4m3":
        byte = np.frexp(amax)[1] - 1 + 127 - 7
    else:
        mant, ex = np.frexp(amax / 6.0)
        byte = np.where(mant > 0.5, ex, ex - 1) + 127
    byte = np.clip(np.where(amax > 0, byte, 1), 1, 254)
    scaled = (w * np.exp2(127.0 - byte)[:, None, :]).reshape(k, n).astype(np.float32)
    by_word = np.ascontiguousarray(scaled.reshape(k // 512, 128, 4, n).transpose(0, 1, 3, 2))
    if fmt == "e4m3":
        words = by_word.astype(ml_dtypes.float8_e4m3fn).view(np.uint8)
    else:
        c = by_word.astype(ml_dtypes.float4_e2m1fn).view(np.uint8) & 0xF
        words = (c[..., 0::2] | (c[..., 1::2] << 4)).reshape(k // 512, 128, 2 * n)
    return np.ascontiguousarray(words), np.ascontiguousarray(byte.astype(np.uint8).reshape(k // 512, 16, n))


def unpack_weight(words, scales, fmt):
    g, _, n = scales.shape
    words = np.ascontiguousarray(words).reshape(g, 128, n, -1)
    if fmt == "e4m3":
        vals = words.view(ml_dtypes.float8_e4m3fn).astype(np.float64)
    else:
        nib = np.empty((g, 128, n, 4), np.uint8)
        nib[..., 0::2] = words & 0xF
        nib[..., 1::2] = words >> 4
        vals = E2M1[nib]
    vals = vals * np.repeat(np.exp2(scales.astype(np.float64) - 127.0), 8, axis=1)[..., None]
    return vals.transpose(0, 1, 3, 2).reshape(g * 512, n)


D, T, I, J, Q = 512, 2048, 1024, 512, 128


def setup_inputs():
    n = np.random.standard_normal
    idx = np.random.permutation(T)[:I]
    idx2 = np.random.randint(0, I, J)
    idx3 = np.random.randint(0, I, J)
    fd = mx_kscale(D)
    tokp = pack_weight(n((D, T)) / fd[:, None], "e4m3")
    return {
        "qs": (n((D, Q)) * 0.8 / np.sqrt(D) * fd[:, None]).astype(np.float32),
        "qe": (n((D, Q)) * 0.8 / np.sqrt(D) * fd[:, None]).astype(np.float32),
        "tok_words": tokp[0],
        "tok_scales": tokp[1],
        "offs": striped(idx),
        "offs2": striped(idx2),
        "offs3": striped(idx3),
    }


def reference(qs, qe, tok_words, tok_scales, offs, offs2, offs3):
    idx = unstriped(offs)
    idx2 = unstriped(offs2)
    idx3 = unstriped(offs3)
    toku = unpack_weight(tok_words, tok_scales, "e4m3")
    qsq = mxq(f64(qs), 0, "e4m3")
    tokidxg = toku[:, idx]
    a = qsq.T @ tokidxg
    qeq = mxq(f64(qe), 0, "e4m3")
    b = qeq.T @ tokidxg
    s = a[:, idx2] + b[:, idx3]
    p = np.exp(s - np.max(s, axis=1, keepdims=True))
    y = p / np.sum(p, axis=1, keepdims=True) * 512.0
    return y

@@ -1,0 +1,119 @@
+from contextlib import ExitStack
+
+import concourse.mybir as mybir
+
+F32 = mybir.dt.float32
+BF16 = mybir.dt.bfloat16
+I32 = mybir.dt.int32
+U32 = mybir.dt.uint32
+U16 = mybir.dt.uint16
+U8 = mybir.dt.uint8
+FP8X4 = mybir.dt.float8_e4m3fn_x4
+ALU = mybir.AluOpType
+ACT = mybir.ActivationFunctionType
+AXIS = mybir.AxisListType
+
+P = 128
+PACK = 4
+D, T, I, J, Q = 512, 2048, 1024, 512, 128
+PER_COLUMN = 16
+SLOT_PIECE = 256
+SPAN_PIECE = 256
+OUT_SCALE = 512.0
+FLOPS = 2 * 2 * D * Q * I
+
+
+def tile_attend_spanpointer_kernel(tc, qs, qe, tok_words, tok_scales, offs, offs2, offs3, out):
+    nc = tc.nc
+    n_slot = I // SLOT_PIECE
+    n_span = J // SPAN_PIECE
+    with ExitStack() as ctx:
+        sb = ctx.enter_context(tc.tile_pool(name="sb", bufs=1))
+        ps = ctx.enter_context(tc.psum_pool(name="ps", bufs=1))
+
+        slot_list = sb.tile([P, I // PER_COLUMN], U16, name="slot_list")
+        start_list = sb.tile([P, J // PER_COLUMN], U16, name="start_list")
+        end_list = sb.tile([P, J // PER_COLUMN], U16, name="end_list")
+        words = sb.tile([P, T], I32, name="words", align_bytes=64)
+        scales = sb.tile([P, T], U8, name="scales", align_bytes=64)
+        qs_raw = sb.tile([P, PACK, Q], F32, name="qs_raw", align_bytes=64)
+        qe_raw = sb.tile([P, PACK, Q], F32, name="qe_raw", align_bytes=64)
+
+        nc.vector.memset(scales[:].bitcast(I32), 0)
+        scale_rows = tok_scales[0].bitcast(I32)
+        for r in range(PACK):
+            nc.scalar.dma_start(scales[r:P:32, :].bitcast(I32), scale_rows[r:16:PACK, :])
+
+        nc.sync.dma_start(slot_list[:], offs)
+        nc.sync.dma_start(start_list[:], offs2)
+        nc.sync.dma_start(qs_raw[:], qs.rearrange("(p t) q -> p t q", t=PACK))
+        nc.sync.dma_start(qe_raw[:], qe.rearrange("(p t) q -> p t q", t=PACK))
+        nc.sync.dma_start(words[:], tok_words[0].rearrange("p n t -> p (n t)").bitcast(I32))
+        nc.sync.dma_start(end_list[:], offs3)
+
+        q_grouped = sb.tile([P, 2, Q, PACK], BF16, name="q_grouped", align_bytes=64)
+        for h, (raw, copy) in enumerate(((qs_raw, nc.vector.tensor_copy), (qe_raw, nc.scalar.copy))):
+            copy(
+                q_grouped[:, h].rearrange("p (c i) t -> p c t i", i=4),
+                raw[:].rearrange("p t (c i) -> p c t i", i=4),
+            )
+
+        tok_plane = sb.tile([P, I], U8, name="tok_plane", align_bytes=64)
+        nc.vector.tensor_copy(tok_plane[:], scales[:].indirect(slot_list[:]))
+
+        q_codes = sb.tile([P, 2 * Q], U32, name="q_codes", align_bytes=64)
+        q_plane = sb.tile([P, 2 * Q], U8, name="q_plane", align_bytes=64)
+        nc.vector.quantize_mx(q_codes[:].bitcast(FP8X4), q_plane[:], q_grouped[:].rearrange("p h q t -> p (h q t)"))
+
+        tok_codes = []
+        cols = SLOT_PIECE // PER_COLUMN
+        for u in range(n_slot):
+            piece = sb.tile([P, SLOT_PIECE], U32, name="tok_codes%d" % u, align_bytes=64)
+            nc.vector.tensor_copy(piece[:], words[:].bitcast(U32).indirect(slot_list[:, u * cols : (u + 1) * cols]))
+            tok_codes.append(piece)
+
+        a_sb = sb.tile([P, I], F32, name="a_sb")
+        b_sb = sb.tile([P, I], F32, name="b_sb")
+        for u in range(n_slot):
+            slots = slice(u * SLOT_PIECE, (u + 1) * SLOT_PIECE)
+            for h, dst in enumerate((a_sb, b_sb)):
+                rows = slice(h * Q, (h + 1) * Q)
+                bank = ps.tile([P, SLOT_PIECE], F32, name="bank%d_%d" % (h, u))
+                nc.tensor.matmul_mx(
+                    bank[:],
+                    lhsT=q_codes[:, rows].bitcast(FP8X4),
+                    lhsT_scale=q_plane[:, rows],
+                    rhs=tok_codes[u][:].bitcast(FP8X4),
+                    rhs_scale=tok_plane[:, slots],
+                    start=True,
+                    stop=True,
+                )
+                if h == 0 and u == n_slot - 1:
+                    nc.vector.tensor_copy(dst[:, slots], bank[:])
+                else:
+                    nc.scalar.copy(dst[:, slots], bank[:])
+
+        a_picked = sb.tile([P, J], F32, name="a_picked")
+        s = sb.tile([P, J], F32, name="s")
+        cols = SPAN_PIECE // PER_COLUMN
+        for v in range(n_span):
+            spans = slice(v * SPAN_PIECE, (v + 1) * SPAN_PIECE)
+            nc.vector.tensor_copy(a_picked[:, spans], a_sb[:].indirect(start_list[:, v * cols : (v + 1) * cols]))
+        for v in range(n_span):
+            spans = slice(v * SPAN_PIECE, (v + 1) * SPAN_PIECE)
+            nc.vector.tensor_tensor(
+                s[:, spans], b_sb[:].indirect(end_list[:, v * cols : (v + 1) * cols]), a_picked[:, spans], ALU.add
+            )
+
+        neg_max = sb.tile([P, 1], F32, name="neg_max")
+        nc.vector.tensor_reduce(neg_max[:], s[:], AXIS.X, ALU.max, negate=True)
+        p = sb.tile([P, J], F32, name="p")
+        row_sum = sb.tile([P, 1], F32, name="row_sum")
+        nc.scalar.activation(p[:], s[:], ACT.Exp, bias=neg_max[:], accum_out=row_sum[:])
+        inv_sum = sb.tile([P, 1], F32, name="inv_sum")
+        nc.vector.reciprocal(inv_sum[:], row_sum[:])
+        y = sb.tile([P, J], F32, name="y")
+        for v in range(n_span):
+            spans = slice(v * SPAN_PIECE, (v + 1) * SPAN_PIECE)
+            nc.vector.tensor_scalar(y[:, spans], p[:, spans], inv_sum[:], OUT_SCALE, ALU.mult, ALU.mult)
+            nc.sync.dma_start(out[:, spans], y[:, spans])

@@ -19,7 +19,6 @@ D, T, I, J, Q = 512, 2048, 1024, 512, 128
 PER_COLUMN = 16
 SLOT_PIECE = 256
 SPAN_PIECE = 256
-OUT_SCALE = 512.0
 FLOPS = 2 * 2 * D * Q * I
 
 
@@ -40,30 +39,37 @@ def tile_attend_spanpointer_kernel(tc, qs, qe, tok_words, tok_scales, offs, offs
         qe_raw = sb.tile([P, PACK, Q], F32, name="qe_raw", align_bytes=64)
 
         nc.vector.memset(scales[:].bitcast(I32), 0)
+
+        nc.sync.dma_start(qs_raw[:], qs.rearrange("(p t) q -> p t q", t=PACK))
+        nc.sync.dma_start(slot_list[:], offs)
         scale_rows = tok_scales[0].bitcast(I32)
         for r in range(PACK):
-            nc.scalar.dma_start(scales[r:P:32, :].bitcast(I32), scale_rows[r:16:PACK, :])
-
-        nc.sync.dma_start(slot_list[:], offs)
-        nc.sync.dma_start(start_list[:], offs2)
-        nc.sync.dma_start(qs_raw[:], qs.rearrange("(p t) q -> p t q", t=PACK))
-        nc.sync.dma_start(qe_raw[:], qe.rearrange("(p t) q -> p t q", t=PACK))
+            nc.sync.dma_start(scales[r:P:32, :].bitcast(I32), scale_rows[r:16:PACK, :])
         nc.sync.dma_start(words[:], tok_words[0].rearrange("p n t -> p (n t)").bitcast(I32))
+        nc.sync.dma_start(qe_raw[:], qe.rearrange("(p t) q -> p t q", t=PACK))
+        nc.sync.dma_start(start_list[:], offs2)
         nc.sync.dma_start(end_list[:], offs3)
 
-        q_grouped = sb.tile([P, 2, Q, PACK], BF16, name="q_grouped", align_bytes=64)
-        for h, (raw, copy) in enumerate(((qs_raw, nc.vector.tensor_copy), (qe_raw, nc.scalar.copy))):
+        def interleave(raw, name, copy):
+            grouped = sb.tile([P, Q, PACK], BF16, name=name + "_grouped", align_bytes=64)
             copy(
-                q_grouped[:, h].rearrange("p (c i) t -> p c t i", i=4),
+                grouped[:].rearrange("p (c i) t -> p c t i", i=4),
                 raw[:].rearrange("p t (c i) -> p c t i", i=4),
             )
+            return grouped
+
+        def quantise(grouped, name):
+            codes = sb.tile([P, Q], U32, name=name + "_codes", align_bytes=64)
+            plane = sb.tile([P, Q], U8, name=name + "_plane", align_bytes=64)
+            nc.vector.quantize_mx(codes[:].bitcast(FP8X4), plane[:], grouped[:].rearrange("p q t -> p (q t)"))
+            return codes, plane
+
+        qs_grouped = interleave(qs_raw, "qs", nc.vector.tensor_copy)
+        qe_grouped = interleave(qe_raw, "qe", nc.scalar.copy)
 
         tok_plane = sb.tile([P, I], U8, name="tok_plane", align_bytes=64)
         nc.vector.tensor_copy(tok_plane[:], scales[:].indirect(slot_list[:]))
-
-        q_codes = sb.tile([P, 2 * Q], U32, name="q_codes", align_bytes=64)
-        q_plane = sb.tile([P, 2 * Q], U8, name="q_plane", align_bytes=64)
-        nc.vector.quantize_mx(q_codes[:].bitcast(FP8X4), q_plane[:], q_grouped[:].rearrange("p h q t -> p (h q t)"))
+        qs_mx = quantise(qs_grouped, "qs")
 
         tok_codes = []
         cols = SLOT_PIECE // PER_COLUMN
@@ -71,27 +77,32 @@ def tile_attend_spanpointer_kernel(tc, qs, qe, tok_words, tok_scales, offs, offs
             piece = sb.tile([P, SLOT_PIECE], U32, name="tok_codes%d" % u, align_bytes=64)
             nc.vector.tensor_copy(piece[:], words[:].bitcast(U32).indirect(slot_list[:, u * cols : (u + 1) * cols]))
             tok_codes.append(piece)
+        qe_mx = quantise(qe_grouped, "qe")
 
         a_sb = sb.tile([P, I], F32, name="a_sb")
         b_sb = sb.tile([P, I], F32, name="b_sb")
-        for u in range(n_slot):
+
+        def score(q_mx, u, dst, name, on_vector):
             slots = slice(u * SLOT_PIECE, (u + 1) * SLOT_PIECE)
-            for h, dst in enumerate((a_sb, b_sb)):
-                rows = slice(h * Q, (h + 1) * Q)
-                bank = ps.tile([P, SLOT_PIECE], F32, name="bank%d_%d" % (h, u))
-                nc.tensor.matmul_mx(
-                    bank[:],
-                    lhsT=q_codes[:, rows].bitcast(FP8X4),
-                    lhsT_scale=q_plane[:, rows],
-                    rhs=tok_codes[u][:].bitcast(FP8X4),
-                    rhs_scale=tok_plane[:, slots],
-                    start=True,
-                    stop=True,
-                )
-                if h == 0 and u == n_slot - 1:
-                    nc.vector.tensor_copy(dst[:, slots], bank[:])
-                else:
-                    nc.scalar.copy(dst[:, slots], bank[:])
+            bank = ps.tile([P, SLOT_PIECE], F32, name="%s_bank%d" % (name, u))
+            nc.tensor.matmul_mx(
+                bank[:],
+                lhsT=q_mx[0][:].bitcast(FP8X4),
+                lhsT_scale=q_mx[1][:],
+                rhs=tok_codes[u][:].bitcast(FP8X4),
+                rhs_scale=tok_plane[:, slots],
+                start=True,
+                stop=True,
+            )
+            if on_vector:
+                nc.vector.tensor_copy(dst[:, slots], bank[:])
+            else:
+                nc.scalar.copy(dst[:, slots], bank[:])
+
+        for u in range(n_slot):
+            score(qs_mx, u, a_sb, "a", False)
+        for u in range(n_slot):
+            score(qe_mx, u, b_sb, "b", False)
 
         a_picked = sb.tile([P, J], F32, name="a_picked")
         s = sb.tile([P, J], F32, name="s")
@@ -115,5 +126,5 @@ def tile_attend_spanpointer_kernel(tc, qs, qe, tok_words, tok_scales, offs, offs
         y = sb.tile([P, J], F32, name="y")
         for v in range(n_span):
             spans = slice(v * SPAN_PIECE, (v + 1) * SPAN_PIECE)
-            nc.vector.tensor_scalar(y[:, spans], p[:, spans], inv_sum[:], OUT_SCALE, ALU.mult, ALU.mult)
+            nc.vector.tensor_scalar(y[:, spans], p[:, spans], inv_sum[:], float(J), ALU.mult, ALU.mult)
             nc.sync.dma_start(out[:, spans], y[:, spans])

@@ -44,32 +44,39 @@ def tile_attend_spanpointer_kernel(tc, qs, qe, tok_words, tok_scales, offs, offs
         nc.sync.dma_start(slot_list[:], offs)
         scale_rows = tok_scales[0].bitcast(I32)
         for r in range(PACK):
-            nc.sync.dma_start(scales[r:P:32, :].bitcast(I32), scale_rows[r:16:PACK, :])
+            queue = nc.sync if r % 2 == 0 else nc.scalar
+            queue.dma_start(scales[r:P:32, :].bitcast(I32), scale_rows[r:16:PACK, :])
         nc.sync.dma_start(words[:], tok_words[0].rearrange("p n t -> p (n t)").bitcast(I32))
         nc.sync.dma_start(qe_raw[:], qe.rearrange("(p t) q -> p t q", t=PACK))
         nc.sync.dma_start(start_list[:], offs2)
         nc.sync.dma_start(end_list[:], offs3)
 
-        def interleave(raw, name, copy):
+        def interleave(raw, name, copy, parts):
             grouped = sb.tile([P, Q, PACK], BF16, name=name + "_grouped", align_bytes=64)
-            copy(
-                grouped[:].rearrange("p (c i) t -> p c t i", i=4),
-                raw[:].rearrange("p t (c i) -> p c t i", i=4),
-            )
+            for first in range(0, Q, Q // parts):
+                rows = slice(first, first + Q // parts)
+                copy(
+                    grouped[:, rows, :].rearrange("p (c i) t -> p c t i", i=4),
+                    raw[:, :, rows].rearrange("p t (c i) -> p c t i", i=4),
+                )
             return grouped
 
-        def quantise(grouped, name):
+        def quantise(grouped, name, parts):
             codes = sb.tile([P, Q], U32, name=name + "_codes", align_bytes=64)
             plane = sb.tile([P, Q], U8, name=name + "_plane", align_bytes=64)
-            nc.vector.quantize_mx(codes[:].bitcast(FP8X4), plane[:], grouped[:].rearrange("p q t -> p (q t)"))
+            for first in range(0, Q, Q // parts):
+                rows = slice(first, first + Q // parts)
+                nc.vector.quantize_mx(
+                    codes[:, rows].bitcast(FP8X4), plane[:, rows], grouped[:, rows, :].rearrange("p q t -> p (q t)")
+                )
             return codes, plane
 
-        qs_grouped = interleave(qs_raw, "qs", nc.vector.tensor_copy)
-        qe_grouped = interleave(qe_raw, "qe", nc.scalar.copy)
+        qs_grouped = interleave(qs_raw, "qs", nc.vector.tensor_copy, 2)
+        qs_mx = quantise(qs_grouped, "qs", 2)
+        qe_grouped = interleave(qe_raw, "qe", nc.scalar.copy, 1)
 
         tok_plane = sb.tile([P, I], U8, name="tok_plane", align_bytes=64)
         nc.vector.tensor_copy(tok_plane[:], scales[:].indirect(slot_list[:]))
-        qs_mx = quantise(qs_grouped, "qs")
 
         tok_codes = []
         cols = SLOT_PIECE // PER_COLUMN
@@ -77,32 +84,31 @@ def tile_attend_spanpointer_kernel(tc, qs, qe, tok_words, tok_scales, offs, offs
             piece = sb.tile([P, SLOT_PIECE], U32, name="tok_codes%d" % u, align_bytes=64)
             nc.vector.tensor_copy(piece[:], words[:].bitcast(U32).indirect(slot_list[:, u * cols : (u + 1) * cols]))
             tok_codes.append(piece)
-        qe_mx = quantise(qe_grouped, "qe")
+        qe_mx = quantise(qe_grouped, "qe", 1)
 
         a_sb = sb.tile([P, I], F32, name="a_sb")
         b_sb = sb.tile([P, I], F32, name="b_sb")
 
-        def score(q_mx, u, dst, name, on_vector):
-            slots = slice(u * SLOT_PIECE, (u + 1) * SLOT_PIECE)
-            bank = ps.tile([P, SLOT_PIECE], F32, name="%s_bank%d" % (name, u))
+        def score(q_mx, dst, first, width, name):
+            u, within = divmod(first, SLOT_PIECE)
+            slots = slice(first, first + width)
+            bank = ps.tile([P, width], F32, name=name, tag="bank", bufs=8)
             nc.tensor.matmul_mx(
                 bank[:],
                 lhsT=q_mx[0][:].bitcast(FP8X4),
                 lhsT_scale=q_mx[1][:],
-                rhs=tok_codes[u][:].bitcast(FP8X4),
+                rhs=tok_codes[u][:, within : within + width].bitcast(FP8X4),
                 rhs_scale=tok_plane[:, slots],
                 start=True,
                 stop=True,
             )
-            if on_vector:
-                nc.vector.tensor_copy(dst[:, slots], bank[:])
-            else:
-                nc.scalar.copy(dst[:, slots], bank[:])
+            nc.scalar.copy(dst[:, slots], bank[:])
 
-        for u in range(n_slot):
-            score(qs_mx, u, a_sb, "a", False)
-        for u in range(n_slot):
-            score(qe_mx, u, b_sb, "b", False)
+        for q_mx, dst, name in ((qs_mx, a_sb, "a_bank"), (qe_mx, b_sb, "b_bank")):
+            for first in range(0, I - SLOT_PIECE, SLOT_PIECE):
+                score(q_mx, dst, first, SLOT_PIECE, name)
+            for first in range(I - SLOT_PIECE, I, SLOT_PIECE // 2):
+                score(q_mx, dst, first, SLOT_PIECE // 2, name)
 
         a_picked = sb.tile([P, J], F32, name="a_picked")
         s = sb.tile([P, J], F32, name="s")

@@ -44,8 +44,7 @@ def tile_attend_spanpointer_kernel(tc, qs, qe, tok_words, tok_scales, offs, offs
         nc.sync.dma_start(slot_list[:], offs)
         scale_rows = tok_scales[0].bitcast(I32)
         for r in range(PACK):
-            queue = nc.sync if r % 2 == 0 else nc.scalar
-            queue.dma_start(scales[r:P:32, :].bitcast(I32), scale_rows[r:16:PACK, :])
+            nc.sync.dma_start(scales[r:P:32, :].bitcast(I32), scale_rows[r:16:PACK, :])
         nc.sync.dma_start(words[:], tok_words[0].rearrange("p n t -> p (n t)").bitcast(I32))
         nc.sync.dma_start(qe_raw[:], qe.rearrange("(p t) q -> p t q", t=PACK))
         nc.sync.dma_start(start_list[:], offs2)

@@ -19,6 +19,7 @@ D, T, I, J, Q = 512, 2048, 1024, 512, 128
 PER_COLUMN = 16
 SLOT_PIECE = 256
 SPAN_PIECE = 256
+STORE_PIECE = 128
 FLOPS = 2 * 2 * D * Q * I
 
 
@@ -129,7 +130,7 @@ def tile_attend_spanpointer_kernel(tc, qs, qe, tok_words, tok_scales, offs, offs
         inv_sum = sb.tile([P, 1], F32, name="inv_sum")
         nc.vector.reciprocal(inv_sum[:], row_sum[:])
         y = sb.tile([P, J], F32, name="y")
-        for v in range(n_span):
-            spans = slice(v * SPAN_PIECE, (v + 1) * SPAN_PIECE)
+        for v in range(J // STORE_PIECE):
+            spans = slice(v * STORE_PIECE, (v + 1) * STORE_PIECE)
             nc.vector.tensor_scalar(y[:, spans], p[:, spans], inv_sum[:], float(J), ALU.mult, ALU.mult)
-            nc.sync.dma_start(out[:, spans], y[:, spans])
+            (nc.sync, nc.scalar)[v % 2].dma_start(out[:, spans], y[:, spans])

@@ -20,6 +20,7 @@ PER_COLUMN = 16
 SLOT_PIECE = 256
 SPAN_PIECE = 256
 STORE_PIECE = 128
+ROW0 = 112
 FLOPS = 2 * 2 * D * Q * I
 
 
@@ -39,13 +40,13 @@ def tile_attend_spanpointer_kernel(tc, qs, qe, tok_words, tok_scales, offs, offs
         qs_raw = sb.tile([P, PACK, Q], F32, name="qs_raw", align_bytes=64)
         qe_raw = sb.tile([P, PACK, Q], F32, name="qe_raw", align_bytes=64)
 
-        nc.vector.memset(scales[:].bitcast(I32), 0)
+        tok_plane = sb.tile([P, I], U8, name="tok_plane", align_bytes=64)
+        nc.vector.memset(scales[:ROW0, :].bitcast(I32), 0)
+        nc.vector.memset(tok_plane[:].bitcast(I32), 0)
 
-        nc.sync.dma_start(qs_raw[:], qs.rearrange("(p t) q -> p t q", t=PACK))
+        nc.sync.dma_start(scales[ROW0:, :].bitcast(I32), tok_scales[0].bitcast(I32))
         nc.sync.dma_start(slot_list[:], offs)
-        scale_rows = tok_scales[0].bitcast(I32)
-        for r in range(PACK):
-            nc.sync.dma_start(scales[r:P:32, :].bitcast(I32), scale_rows[r:16:PACK, :])
+        nc.sync.dma_start(qs_raw[:], qs.rearrange("(p t) q -> p t q", t=PACK))
         nc.sync.dma_start(words[:], tok_words[0].rearrange("p n t -> p (n t)").bitcast(I32))
         nc.sync.dma_start(qe_raw[:], qe.rearrange("(p t) q -> p t q", t=PACK))
         nc.sync.dma_start(start_list[:], offs2)
@@ -71,12 +72,17 @@ def tile_attend_spanpointer_kernel(tc, qs, qe, tok_words, tok_scales, offs, offs
                 )
             return codes, plane
 
-        qs_grouped = interleave(qs_raw, "qs", nc.vector.tensor_copy, 2)
-        qs_mx = quantise(qs_grouped, "qs", 2)
+        qs_grouped = interleave(qs_raw, "qs", nc.scalar.copy, 1)
         qe_grouped = interleave(qe_raw, "qe", nc.scalar.copy, 1)
 
-        tok_plane = sb.tile([P, I], U8, name="tok_plane", align_bytes=64)
-        nc.vector.tensor_copy(tok_plane[:], scales[:].indirect(slot_list[:]))
+        picked = sb.tile([P, I], U8, name="picked", align_bytes=64)
+        nc.vector.tensor_copy(picked[:], scales[:].indirect(slot_list[:]))
+        for quad in (0, 2, 1, 3):
+            nc.sync.dma_start(
+                tok_plane[32 * quad : 32 * quad + PACK, :].bitcast(I32),
+                picked[ROW0 + PACK * quad : ROW0 + PACK * (quad + 1), :].bitcast(I32),
+            )
+        qs_mx = quantise(qs_grouped, "qs", 1)
 
         tok_codes = []
         cols = SLOT_PIECE // PER_COLUMN

@@ -26,7 +26,6 @@ FLOPS = 2 * 2 * D * Q * I
 
 def tile_attend_spanpointer_kernel(tc, qs, qe, tok_words, tok_scales, offs, offs2, offs3, out):
     nc = tc.nc
-    n_slot = I // SLOT_PIECE
     n_span = J // SPAN_PIECE
     with ExitStack() as ctx:
         sb = ctx.enter_context(tc.tile_pool(name="sb", bufs=1))
@@ -37,7 +36,7 @@ def tile_attend_spanpointer_kernel(tc, qs, qe, tok_words, tok_scales, offs, offs
         end_list = sb.tile([P, J // PER_COLUMN], U16, name="end_list")
         words = sb.tile([P, T], I32, name="words", align_bytes=64)
         scales = sb.tile([P, T], U8, name="scales", align_bytes=64)
-        qs_raw = sb.tile([P, PACK, Q], F32, name="qs_raw", align_bytes=64)
+        qs_raw = sb.tile([P, PACK, Q], F32, name="qs_raw", tag="stage", align_bytes=64)
         qe_raw = sb.tile([P, PACK, Q], F32, name="qe_raw", align_bytes=64)
 
         tok_plane = sb.tile([P, I], U8, name="tok_plane", align_bytes=64)
@@ -46,11 +45,11 @@ def tile_attend_spanpointer_kernel(tc, qs, qe, tok_words, tok_scales, offs, offs
 
         nc.sync.dma_start(scales[ROW0:, :].bitcast(I32), tok_scales[0].bitcast(I32))
         nc.sync.dma_start(slot_list[:], offs)
-        nc.sync.dma_start(qs_raw[:], qs.rearrange("(p t) q -> p t q", t=PACK))
         nc.sync.dma_start(words[:], tok_words[0].rearrange("p n t -> p (n t)").bitcast(I32))
-        nc.sync.dma_start(qe_raw[:], qe.rearrange("(p t) q -> p t q", t=PACK))
+        nc.sync.dma_start(qs_raw[:], qs.rearrange("(p t) q -> p t q", t=PACK))
         nc.sync.dma_start(start_list[:], offs2)
         nc.sync.dma_start(end_list[:], offs3)
+        nc.sync.dma_start(qe_raw[:], qe.rearrange("(p t) q -> p t q", t=PACK))
 
         def interleave(raw, name, copy, parts):
             grouped = sb.tile([P, Q, PACK], BF16, name=name + "_grouped", align_bytes=64)
@@ -75,46 +74,53 @@ def tile_attend_spanpointer_kernel(tc, qs, qe, tok_words, tok_scales, offs, offs
         qs_grouped = interleave(qs_raw, "qs", nc.scalar.copy, 1)
         qe_grouped = interleave(qe_raw, "qe", nc.scalar.copy, 1)
 
-        picked = sb.tile([P, I], U8, name="picked", align_bytes=64)
-        nc.vector.tensor_copy(picked[:], scales[:].indirect(slot_list[:]))
-        for quad in (0, 2, 1, 3):
-            nc.sync.dma_start(
-                tok_plane[32 * quad : 32 * quad + PACK, :].bitcast(I32),
-                picked[ROW0 + PACK * quad : ROW0 + PACK * (quad + 1), :].bitcast(I32),
+        for first, last in ((0, I - SLOT_PIECE), (I - SLOT_PIECE, I)):
+            picked = sb.tile([P, last - first], U8, name="picked%d" % first, align_bytes=64)
+            nc.vector.tensor_copy(
+                picked[:], scales[:].indirect(slot_list[:, first // PER_COLUMN : last // PER_COLUMN])
             )
-        qs_mx = quantise(qs_grouped, "qs", 1)
-
+            for quad in (0, 2, 1, 3):
+                nc.sync.dma_start(
+                    tok_plane[32 * quad : 32 * quad + PACK, first:last].bitcast(I32),
+                    picked[ROW0 + PACK * quad : ROW0 + PACK * (quad + 1), :].bitcast(I32),
+                )
         tok_codes = []
-        cols = SLOT_PIECE // PER_COLUMN
-        for u in range(n_slot):
-            piece = sb.tile([P, SLOT_PIECE], U32, name="tok_codes%d" % u, align_bytes=64)
-            nc.vector.tensor_copy(piece[:], words[:].bitcast(U32).indirect(slot_list[:, u * cols : (u + 1) * cols]))
-            tok_codes.append(piece)
+
+        def gather_words(first, last, tag):
+            piece = sb.tile([P, last - first], U32, name="tok_codes%d" % first, tag=tag, align_bytes=64)
+            nc.vector.tensor_copy(
+                piece[:], words[:].bitcast(U32).indirect(slot_list[:, first // PER_COLUMN : last // PER_COLUMN])
+            )
+            tok_codes.append((first, last, piece))
+
+        gather_words(0, 384, "codes0")
+        gather_words(384, 640, "codes1")
+        qs_mx = quantise(qs_grouped, "qs", 1)
+        gather_words(640, I, "stage")
         qe_mx = quantise(qe_grouped, "qe", 1)
 
         a_sb = sb.tile([P, I], F32, name="a_sb")
         b_sb = sb.tile([P, I], F32, name="b_sb")
 
         def score(q_mx, dst, first, width, name):
-            u, within = divmod(first, SLOT_PIECE)
+            base, piece = [(lo, tile) for lo, hi, tile in tok_codes if lo <= first < hi][0]
             slots = slice(first, first + width)
             bank = ps.tile([P, width], F32, name=name, tag="bank", bufs=8)
             nc.tensor.matmul_mx(
                 bank[:],
                 lhsT=q_mx[0][:].bitcast(FP8X4),
                 lhsT_scale=q_mx[1][:],
-                rhs=tok_codes[u][:, within : within + width].bitcast(FP8X4),
+                rhs=piece[:, first - base : first - base + width].bitcast(FP8X4),
                 rhs_scale=tok_plane[:, slots],
                 start=True,
                 stop=True,
             )
             nc.scalar.copy(dst[:, slots], bank[:])
 
-        for q_mx, dst, name in ((qs_mx, a_sb, "a_bank"), (qe_mx, b_sb, "b_bank")):
-            for first in range(0, I - SLOT_PIECE, SLOT_PIECE):
-                score(q_mx, dst, first, SLOT_PIECE, name)
-            for first in range(I - SLOT_PIECE, I, SLOT_PIECE // 2):
-                score(q_mx, dst, first, SLOT_PIECE // 2, name)
+        for first, width in ((0, 256), (256, 128), (384, 256), (640, 128), (768, 128), (896, 128)):
+            score(qs_mx, a_sb, first, width, "a_bank")
+        for first, width in ((0, 128), (128, 256), (384, 256), (640, 256), (896, 128)):
+            score(qe_mx, b_sb, first, width, "b_bank")
 
         a_picked = sb.tile([P, J], F32, name="a_picked")
         s = sb.tile([P, J], F32, name="s")

@@ -74,16 +74,14 @@ def tile_attend_spanpointer_kernel(tc, qs, qe, tok_words, tok_scales, offs, offs
         qs_grouped = interleave(qs_raw, "qs", nc.scalar.copy, 1)
         qe_grouped = interleave(qe_raw, "qe", nc.scalar.copy, 1)
 
-        for first, last in ((0, I - SLOT_PIECE), (I - SLOT_PIECE, I)):
-            picked = sb.tile([P, last - first], U8, name="picked%d" % first, align_bytes=64)
-            nc.vector.tensor_copy(
-                picked[:], scales[:].indirect(slot_list[:, first // PER_COLUMN : last // PER_COLUMN])
+        picked = sb.tile([P, I], U8, name="picked", align_bytes=64)
+        nc.vector.tensor_copy(picked[:], scales[:].indirect(slot_list[:]))
+        for quad in (0, 2, 1, 3):
+            nc.sync.dma_start(
+                tok_plane[32 * quad : 32 * quad + PACK, :].bitcast(I32),
+                picked[ROW0 + PACK * quad : ROW0 + PACK * (quad + 1), :].bitcast(I32),
             )
-            for quad in (0, 2, 1, 3):
-                nc.sync.dma_start(
-                    tok_plane[32 * quad : 32 * quad + PACK, first:last].bitcast(I32),
-                    picked[ROW0 + PACK * quad : ROW0 + PACK * (quad + 1), :].bitcast(I32),
-                )
+
         tok_codes = []
 
         def gather_words(first, last, tag):
@@ -93,8 +91,7 @@ def tile_attend_spanpointer_kernel(tc, qs, qe, tok_words, tok_scales, offs, offs
             )
             tok_codes.append((first, last, piece))
 
-        gather_words(0, 384, "codes0")
-        gather_words(384, 640, "codes1")
+        gather_words(0, 640, "codes0")
         qs_mx = quantise(qs_grouped, "qs", 1)
         gather_words(640, I, "stage")
         qe_mx = quantise(qe_grouped, "qe", 1)
@@ -117,7 +114,7 @@ def tile_attend_spanpointer_kernel(tc, qs, qe, tok_words, tok_scales, offs, offs
             )
             nc.scalar.copy(dst[:, slots], bank[:])
 
-        for first, width in ((0, 256), (256, 128), (384, 256), (640, 128), (768, 128), (896, 128)):
+        for first, width in ((0, 128), (128, 256), (384, 256), (640, 128), (768, 128), (896, 128)):
             score(qs_mx, a_sb, first, width, "a_bank")
         for first, width in ((0, 128), (128, 256), (384, 256), (640, 256), (896, 128)):
             score(qe_mx, b_sb, first, width, "b_bank")

@@ -43,13 +43,13 @@ def tile_attend_spanpointer_kernel(tc, qs, qe, tok_words, tok_scales, offs, offs
         nc.vector.memset(scales[:ROW0, :].bitcast(I32), 0)
         nc.vector.memset(tok_plane[:].bitcast(I32), 0)
 
-        nc.sync.dma_start(scales[ROW0:, :].bitcast(I32), tok_scales[0].bitcast(I32))
+        nc.scalar.dma_start(scales[ROW0:, :].bitcast(I32), tok_scales[0].bitcast(I32))
         nc.sync.dma_start(slot_list[:], offs)
         nc.sync.dma_start(words[:], tok_words[0].rearrange("p n t -> p (n t)").bitcast(I32))
         nc.sync.dma_start(qs_raw[:], qs.rearrange("(p t) q -> p t q", t=PACK))
+        nc.sync.dma_start(qe_raw[:], qe.rearrange("(p t) q -> p t q", t=PACK))
         nc.sync.dma_start(start_list[:], offs2)
         nc.sync.dma_start(end_list[:], offs3)
-        nc.sync.dma_start(qe_raw[:], qe.rearrange("(p t) q -> p t q", t=PACK))
 
         def interleave(raw, name, copy, parts):
             grouped = sb.tile([P, Q, PACK], BF16, name=name + "_grouped", align_bytes=64)

@@ -17,19 +17,24 @@ P = 128
 PACK = 4
 D, T, I, J, Q = 512, 2048, 1024, 512, 128
 PER_COLUMN = 16
-SLOT_PIECE = 256
+QUADRANT = 32
+SCALE_ROW0 = 112
 SPAN_PIECE = 256
 STORE_PIECE = 128
-ROW0 = 112
+EARLY_SLOTS = 512
+QS_ON_SCALAR = 96
+QE_ON_SCALAR = 128
 FLOPS = 2 * 2 * D * Q * I
 
 
 def tile_attend_spanpointer_kernel(tc, qs, qe, tok_words, tok_scales, offs, offs2, offs3, out):
     nc = tc.nc
-    n_span = J // SPAN_PIECE
     with ExitStack() as ctx:
         sb = ctx.enter_context(tc.tile_pool(name="sb", bufs=1))
         ps = ctx.enter_context(tc.psum_pool(name="ps", bufs=1))
+
+        def columns(first, last):
+            return slice(first // PER_COLUMN, last // PER_COLUMN)
 
         slot_list = sb.tile([P, I // PER_COLUMN], U16, name="slot_list")
         start_list = sb.tile([P, J // PER_COLUMN], U16, name="start_list")
@@ -38,12 +43,12 @@ def tile_attend_spanpointer_kernel(tc, qs, qe, tok_words, tok_scales, offs, offs
         scales = sb.tile([P, T], U8, name="scales", align_bytes=64)
         qs_raw = sb.tile([P, PACK, Q], F32, name="qs_raw", tag="stage", align_bytes=64)
         qe_raw = sb.tile([P, PACK, Q], F32, name="qe_raw", align_bytes=64)
-
         tok_plane = sb.tile([P, I], U8, name="tok_plane", align_bytes=64)
-        nc.vector.memset(scales[:ROW0, :].bitcast(I32), 0)
+
+        nc.vector.memset(scales[:SCALE_ROW0, :].bitcast(I32), 0)
         nc.vector.memset(tok_plane[:].bitcast(I32), 0)
 
-        nc.scalar.dma_start(scales[ROW0:, :].bitcast(I32), tok_scales[0].bitcast(I32))
+        nc.scalar.dma_start(scales[SCALE_ROW0:, :].bitcast(I32), tok_scales[0].bitcast(I32))
         nc.sync.dma_start(slot_list[:], offs)
         nc.sync.dma_start(words[:], tok_words[0].rearrange("p n t -> p (n t)").bitcast(I32))
         nc.sync.dma_start(qs_raw[:], qs.rearrange("(p t) q -> p t q", t=PACK))
@@ -51,84 +56,90 @@ def tile_attend_spanpointer_kernel(tc, qs, qe, tok_words, tok_scales, offs, offs
         nc.sync.dma_start(start_list[:], offs2)
         nc.sync.dma_start(end_list[:], offs3)
 
-        def interleave(raw, name, copy, parts):
+        def interleave(raw, name, on_scalar):
             grouped = sb.tile([P, Q, PACK], BF16, name=name + "_grouped", align_bytes=64)
-            for first in range(0, Q, Q // parts):
-                rows = slice(first, first + Q // parts)
-                copy(
-                    grouped[:, rows, :].rearrange("p (c i) t -> p c t i", i=4),
-                    raw[:, :, rows].rearrange("p t (c i) -> p c t i", i=4),
+            if on_scalar < Q:
+                nc.gpsimd.tensor_scalar(
+                    grouped[:, on_scalar:, :],
+                    raw[:, :, on_scalar:].rearrange("p t q -> p q t"),
+                    1.0,
+                    0.0,
+                    ALU.mult,
+                    ALU.add,
+                )
+            if on_scalar > 0:
+                nc.scalar.copy(
+                    grouped[:, :on_scalar, :].rearrange("p (c i) t -> p c t i", i=4),
+                    raw[:, :, :on_scalar].rearrange("p t (c i) -> p c t i", i=4),
                 )
             return grouped
 
-        def quantise(grouped, name, parts):
+        def quantise(grouped, name):
             codes = sb.tile([P, Q], U32, name=name + "_codes", align_bytes=64)
             plane = sb.tile([P, Q], U8, name=name + "_plane", align_bytes=64)
-            for first in range(0, Q, Q // parts):
-                rows = slice(first, first + Q // parts)
-                nc.vector.quantize_mx(
-                    codes[:, rows].bitcast(FP8X4), plane[:, rows], grouped[:, rows, :].rearrange("p q t -> p (q t)")
-                )
+            nc.vector.quantize_mx(codes[:].bitcast(FP8X4), plane[:], grouped[:].rearrange("p q t -> p (q t)"))
             return codes, plane
 
-        qs_grouped = interleave(qs_raw, "qs", nc.scalar.copy, 1)
-        qe_grouped = interleave(qe_raw, "qe", nc.scalar.copy, 1)
+        qs_grouped = interleave(qs_raw, "qs", QS_ON_SCALAR)
+        qe_grouped = interleave(qe_raw, "qe", QE_ON_SCALAR)
 
         picked = sb.tile([P, I], U8, name="picked", align_bytes=64)
         nc.vector.tensor_copy(picked[:], scales[:].indirect(slot_list[:]))
         for quad in (0, 2, 1, 3):
             nc.sync.dma_start(
-                tok_plane[32 * quad : 32 * quad + PACK, :].bitcast(I32),
-                picked[ROW0 + PACK * quad : ROW0 + PACK * (quad + 1), :].bitcast(I32),
+                tok_plane[QUADRANT * quad : QUADRANT * quad + PACK, :].bitcast(I32),
+                picked[SCALE_ROW0 + PACK * quad : SCALE_ROW0 + PACK * (quad + 1), :].bitcast(I32),
             )
 
-        tok_codes = []
+        early_codes = sb.tile([P, EARLY_SLOTS], U32, name="early_codes", align_bytes=64)
+        late_codes = sb.tile([P, I - EARLY_SLOTS], U32, name="late_codes", tag="stage", align_bytes=64)
 
-        def gather_words(first, last, tag):
-            piece = sb.tile([P, last - first], U32, name="tok_codes%d" % first, tag=tag, align_bytes=64)
+        def codes_of(first, last):
+            if first < EARLY_SLOTS:
+                return early_codes[:, first:last]
+            return late_codes[:, first - EARLY_SLOTS : last - EARLY_SLOTS]
+
+        def gather_words(first, last):
             nc.vector.tensor_copy(
-                piece[:], words[:].bitcast(U32).indirect(slot_list[:, first // PER_COLUMN : last // PER_COLUMN])
+                codes_of(first, last), words[:].bitcast(U32).indirect(slot_list[:, columns(first, last)])
             )
-            tok_codes.append((first, last, piece))
 
-        gather_words(0, 640, "codes0")
-        qs_mx = quantise(qs_grouped, "qs", 1)
-        gather_words(640, I, "stage")
-        qe_mx = quantise(qe_grouped, "qe", 1)
+        gather_words(0, EARLY_SLOTS)
+        qs_mx = quantise(qs_grouped, "qs")
+        gather_words(512, 768)
+        gather_words(768, 1024)
+        qe_mx = quantise(qe_grouped, "qe")
 
-        a_sb = sb.tile([P, I], F32, name="a_sb")
-        b_sb = sb.tile([P, I], F32, name="b_sb")
+        def score(q_mx, name, widths):
+            table = sb.tile([P, I], F32, name=name)
+            first = 0
+            for width in widths:
+                bank = ps.tile([P, width], F32, name=name + "_bank", tag="bank", bufs=8)
+                nc.tensor.matmul_mx(
+                    bank[:],
+                    lhsT=q_mx[0][:].bitcast(FP8X4),
+                    lhsT_scale=q_mx[1][:],
+                    rhs=codes_of(first, first + width).bitcast(FP8X4),
+                    rhs_scale=tok_plane[:, first : first + width],
+                    start=True,
+                    stop=True,
+                )
+                nc.scalar.copy(table[:, first : first + width], bank[:])
+                first = first + width
+            return table
 
-        def score(q_mx, dst, first, width, name):
-            base, piece = [(lo, tile) for lo, hi, tile in tok_codes if lo <= first < hi][0]
-            slots = slice(first, first + width)
-            bank = ps.tile([P, width], F32, name=name, tag="bank", bufs=8)
-            nc.tensor.matmul_mx(
-                bank[:],
-                lhsT=q_mx[0][:].bitcast(FP8X4),
-                lhsT_scale=q_mx[1][:],
-                rhs=piece[:, first - base : first - base + width].bitcast(FP8X4),
-                rhs_scale=tok_plane[:, slots],
-                start=True,
-                stop=True,
-            )
-            nc.scalar.copy(dst[:, slots], bank[:])
-
-        for first, width in ((0, 128), (128, 256), (384, 256), (640, 128), (768, 128), (896, 128)):
-            score(qs_mx, a_sb, first, width, "a_bank")
-        for first, width in ((0, 128), (128, 256), (384, 256), (640, 256), (896, 128)):
-            score(qe_mx, b_sb, first, width, "b_bank")
+        a_sb = score(qs_mx, "a_sb", (128, 128, 256, 256, 128, 128))
+        b_sb = score(qe_mx, "b_sb", (128, 128, 256, 256, 256))
 
         a_picked = sb.tile([P, J], F32, name="a_picked")
         s = sb.tile([P, J], F32, name="s")
-        cols = SPAN_PIECE // PER_COLUMN
-        for v in range(n_span):
-            spans = slice(v * SPAN_PIECE, (v + 1) * SPAN_PIECE)
-            nc.vector.tensor_copy(a_picked[:, spans], a_sb[:].indirect(start_list[:, v * cols : (v + 1) * cols]))
-        for v in range(n_span):
-            spans = slice(v * SPAN_PIECE, (v + 1) * SPAN_PIECE)
+        for first in range(0, J, SPAN_PIECE):
+            last = first + SPAN_PIECE
+            nc.vector.tensor_copy(a_picked[:, first:last], a_sb[:].indirect(start_list[:, columns(first, last)]))
+        for first in range(0, J, SPAN_PIECE):
+            last = first + SPAN_PIECE
             nc.vector.tensor_tensor(
-                s[:, spans], b_sb[:].indirect(end_list[:, v * cols : (v + 1) * cols]), a_picked[:, spans], ALU.add
+                s[:, first:last], b_sb[:].indirect(end_list[:, columns(first, last)]), a_picked[:, first:last], ALU.add
             )
 
         neg_max = sb.tile([P, 1], F32, name="neg_max")

@@ -21,9 +21,7 @@ QUADRANT = 32
 SCALE_ROW0 = 112
 SPAN_PIECE = 256
 STORE_PIECE = 128
-EARLY_SLOTS = 512
-QS_ON_SCALAR = 96
-QE_ON_SCALAR = 128
+EARLY_SLOTS = 640
 FLOPS = 2 * 2 * D * Q * I
 
 
@@ -48,7 +46,7 @@ def tile_attend_spanpointer_kernel(tc, qs, qe, tok_words, tok_scales, offs, offs
         nc.vector.memset(scales[:SCALE_ROW0, :].bitcast(I32), 0)
         nc.vector.memset(tok_plane[:].bitcast(I32), 0)
 
-        nc.scalar.dma_start(scales[SCALE_ROW0:, :].bitcast(I32), tok_scales[0].bitcast(I32))
+        nc.sync.dma_start(scales[SCALE_ROW0:, :].bitcast(I32), tok_scales[0].bitcast(I32))
         nc.sync.dma_start(slot_list[:], offs)
         nc.sync.dma_start(words[:], tok_words[0].rearrange("p n t -> p (n t)").bitcast(I32))
         nc.sync.dma_start(qs_raw[:], qs.rearrange("(p t) q -> p t q", t=PACK))
@@ -56,22 +54,11 @@ def tile_attend_spanpointer_kernel(tc, qs, qe, tok_words, tok_scales, offs, offs
         nc.sync.dma_start(start_list[:], offs2)
         nc.sync.dma_start(end_list[:], offs3)
 
-        def interleave(raw, name, on_scalar):
+        def interleave(raw, name):
             grouped = sb.tile([P, Q, PACK], BF16, name=name + "_grouped", align_bytes=64)
-            if on_scalar < Q:
-                nc.gpsimd.tensor_scalar(
-                    grouped[:, on_scalar:, :],
-                    raw[:, :, on_scalar:].rearrange("p t q -> p q t"),
-                    1.0,
-                    0.0,
-                    ALU.mult,
-                    ALU.add,
-                )
-            if on_scalar > 0:
-                nc.scalar.copy(
-                    grouped[:, :on_scalar, :].rearrange("p (c i) t -> p c t i", i=4),
-                    raw[:, :, :on_scalar].rearrange("p t (c i) -> p c t i", i=4),
-                )
+            nc.scalar.copy(
+                grouped[:].rearrange("p (c i) t -> p c t i", i=4), raw[:].rearrange("p t (c i) -> p c t i", i=4)
+            )
             return grouped
 
         def quantise(grouped, name):
@@ -80,8 +67,8 @@ def tile_attend_spanpointer_kernel(tc, qs, qe, tok_words, tok_scales, offs, offs
             nc.vector.quantize_mx(codes[:].bitcast(FP8X4), plane[:], grouped[:].rearrange("p q t -> p (q t)"))
             return codes, plane
 
-        qs_grouped = interleave(qs_raw, "qs", QS_ON_SCALAR)
-        qe_grouped = interleave(qe_raw, "qe", QE_ON_SCALAR)
+        qs_grouped = interleave(qs_raw, "qs")
+        qe_grouped = interleave(qe_raw, "qe")
 
         picked = sb.tile([P, I], U8, name="picked", align_bytes=64)
         nc.vector.tensor_copy(picked[:], scales[:].indirect(slot_list[:]))
@@ -106,8 +93,7 @@ def tile_attend_spanpointer_kernel(tc, qs, qe, tok_words, tok_scales, offs, offs
 
         gather_words(0, EARLY_SLOTS)
         qs_mx = quantise(qs_grouped, "qs")
-        gather_words(512, 768)
-        gather_words(768, 1024)
+        gather_words(640, 1024)
         qe_mx = quantise(qe_grouped, "qe")
 
         def score(q_mx, name, widths):
@@ -128,8 +114,8 @@ def tile_attend_spanpointer_kernel(tc, qs, qe, tok_words, tok_scales, offs, offs
                 first = first + width
             return table
 
-        a_sb = score(qs_mx, "a_sb", (128, 128, 256, 256, 128, 128))
-        b_sb = score(qe_mx, "b_sb", (128, 128, 256, 256, 256))
+        a_sb = score(qs_mx, "a_sb", (128, 256, 256, 128, 128, 128))
+        b_sb = score(qe_mx, "b_sb", (128, 256, 256, 256, 128))
 
         a_picked = sb.tile([P, J], F32, name="a_picked")
         s = sb.tile([P, J], F32, name="s")

@@ -46,7 +46,7 @@ def tile_attend_spanpointer_kernel(tc, qs, qe, tok_words, tok_scales, offs, offs
         nc.vector.memset(scales[:SCALE_ROW0, :].bitcast(I32), 0)
         nc.vector.memset(tok_plane[:].bitcast(I32), 0)
 
-        nc.sync.dma_start(scales[SCALE_ROW0:, :].bitcast(I32), tok_scales[0].bitcast(I32))
+        nc.scalar.dma_start(scales[SCALE_ROW0:, :].bitcast(I32), tok_scales[0].bitcast(I32))
         nc.sync.dma_start(slot_list[:], offs)
         nc.sync.dma_start(words[:], tok_words[0].rearrange("p n t -> p (n t)").bitcast(I32))
         nc.sync.dma_start(qs_raw[:], qs.rearrange("(p t) q -> p t q", t=PACK))
@@ -72,10 +72,10 @@ def tile_attend_spanpointer_kernel(tc, qs, qe, tok_words, tok_scales, offs, offs
 
         picked = sb.tile([P, I], U8, name="picked", align_bytes=64)
         nc.vector.tensor_copy(picked[:], scales[:].indirect(slot_list[:]))
-        for quad in (0, 2, 1, 3):
+        for quad, first, last in ((0, 0, I), (2, 0, I), (1, 0, I), (3, I // 2, I), (3, 0, I // 2)):
             nc.sync.dma_start(
-                tok_plane[QUADRANT * quad : QUADRANT * quad + PACK, :].bitcast(I32),
-                picked[SCALE_ROW0 + PACK * quad : SCALE_ROW0 + PACK * (quad + 1), :].bitcast(I32),
+                tok_plane[QUADRANT * quad : QUADRANT * quad + PACK, first:last].bitcast(I32),
+                picked[SCALE_ROW0 + PACK * quad : SCALE_ROW0 + PACK * (quad + 1), first:last].bitcast(I32),
             )
 
         early_codes = sb.tile([P, EARLY_SLOTS], U32, name="early_codes", align_bytes=64)

@@ -72,10 +72,10 @@ def tile_attend_spanpointer_kernel(tc, qs, qe, tok_words, tok_scales, offs, offs
 
         picked = sb.tile([P, I], U8, name="picked", align_bytes=64)
         nc.vector.tensor_copy(picked[:], scales[:].indirect(slot_list[:]))
-        for quad, first, last in ((0, 0, I), (2, 0, I), (1, 0, I), (3, I // 2, I), (3, 0, I // 2)):
+        for quad in (0, 2, 1, 3):
             nc.sync.dma_start(
-                tok_plane[QUADRANT * quad : QUADRANT * quad + PACK, first:last].bitcast(I32),
-                picked[SCALE_ROW0 + PACK * quad : SCALE_ROW0 + PACK * (quad + 1), first:last].bitcast(I32),
+                tok_plane[QUADRANT * quad : QUADRANT * quad + PACK, :].bitcast(I32),
+                picked[SCALE_ROW0 + PACK * quad : SCALE_ROW0 + PACK * (quad + 1), :].bitcast(I32),
             )
 
         early_codes = sb.tile([P, EARLY_SLOTS], U32, name="early_codes", align_bytes=64)
@@ -115,7 +115,7 @@ def tile_attend_spanpointer_kernel(tc, qs, qe, tok_words, tok_scales, offs, offs
             return table
 
         a_sb = score(qs_mx, "a_sb", (128, 256, 256, 128, 128, 128))
-        b_sb = score(qe_mx, "b_sb", (128, 256, 256, 256, 128))
+        b_sb = score(qe_mx, "b_sb", (128,) * (I // 128))
 
         a_picked = sb.tile([P, J], F32, name="a_picked")
         s = sb.tile([P, J], F32, name="s")

@@ -44,7 +44,8 @@ def tile_attend_spanpointer_kernel(tc, qs, qe, tok_words, tok_scales, offs, offs
         tok_plane = sb.tile([P, I], U8, name="tok_plane", align_bytes=64)
 
         nc.vector.memset(scales[:SCALE_ROW0, :].bitcast(I32), 0)
-        nc.vector.memset(tok_plane[:].bitcast(I32), 0)
+        nc.vector.memset(tok_plane[P - QUADRANT :, :].bitcast(I32), 0)
+        nc.vector.tensor_copy(tok_plane[: P - QUADRANT, :].bitcast(I32), scales[: P - QUADRANT, :I].bitcast(I32))
 
         nc.scalar.dma_start(scales[SCALE_ROW0:, :].bitcast(I32), tok_scales[0].bitcast(I32))
         nc.sync.dma_start(slot_list[:], offs)

@@ -115,7 +115,7 @@ def tile_attend_spanpointer_kernel(tc, qs, qe, tok_words, tok_scales, offs, offs
                 first = first + width
             return table
 
-        a_sb = score(qs_mx, "a_sb", (128, 256, 256, 128, 128, 128))
+        a_sb = score(qs_mx, "a_sb", (128,) * (I // 128))
         b_sb = score(qe_mx, "b_sb", (128,) * (I // 128))
 
         a_picked = sb.tile([P, J], F32, name="a_picked")

@@ -19,9 +19,11 @@ D, T, I, J, Q = 512, 2048, 1024, 512, 128
 PER_COLUMN = 16
 QUADRANT = 32
 SCALE_ROW0 = 112
-SPAN_PIECE = 256
+VECTOR_STARTS = 320
+SCALAR_ENDS = 128
 STORE_PIECE = 128
-EARLY_SLOTS = 640
+CUT_QS = 512
+CUT_QE = 768
 FLOPS = 2 * 2 * D * Q * I
 
 
@@ -39,8 +41,8 @@ def tile_attend_spanpointer_kernel(tc, qs, qe, tok_words, tok_scales, offs, offs
         end_list = sb.tile([P, J // PER_COLUMN], U16, name="end_list")
         words = sb.tile([P, T], I32, name="words", align_bytes=64)
         scales = sb.tile([P, T], U8, name="scales", align_bytes=64)
-        qs_raw = sb.tile([P, PACK, Q], F32, name="qs_raw", tag="stage", align_bytes=64)
-        qe_raw = sb.tile([P, PACK, Q], F32, name="qe_raw", align_bytes=64)
+        qs_raw = sb.tile([P, PACK, Q], F32, name="qs_raw", tag="stage_s", align_bytes=64)
+        qe_raw = sb.tile([P, PACK, Q], F32, name="qe_raw", tag="stage_e", align_bytes=64)
         tok_plane = sb.tile([P, I], U8, name="tok_plane", align_bytes=64)
 
         nc.vector.memset(scales[:SCALE_ROW0, :].bitcast(I32), 0)
@@ -79,55 +81,70 @@ def tile_attend_spanpointer_kernel(tc, qs, qe, tok_words, tok_scales, offs, offs
                 picked[SCALE_ROW0 + PACK * quad : SCALE_ROW0 + PACK * (quad + 1), :].bitcast(I32),
             )
 
-        early_codes = sb.tile([P, EARLY_SLOTS], U32, name="early_codes", align_bytes=64)
-        late_codes = sb.tile([P, I - EARLY_SLOTS], U32, name="late_codes", tag="stage", align_bytes=64)
+        early_codes = sb.tile([P, CUT_QS], U32, name="early_codes", align_bytes=64)
+        middle_codes = sb.tile([P, CUT_QE - CUT_QS], U32, name="middle_codes", tag="stage_s", align_bytes=64)
+        late_codes = sb.tile([P, I - CUT_QE], U32, name="late_codes", tag="stage_e", align_bytes=64)
 
         def codes_of(first, last):
-            if first < EARLY_SLOTS:
+            if first < CUT_QS:
                 return early_codes[:, first:last]
-            return late_codes[:, first - EARLY_SLOTS : last - EARLY_SLOTS]
+            if first < CUT_QE:
+                return middle_codes[:, first - CUT_QS : last - CUT_QS]
+            return late_codes[:, first - CUT_QE : last - CUT_QE]
 
         def gather_words(first, last):
             nc.vector.tensor_copy(
                 codes_of(first, last), words[:].bitcast(U32).indirect(slot_list[:, columns(first, last)])
             )
 
-        gather_words(0, EARLY_SLOTS)
+        gather_words(0, CUT_QS)
         qs_mx = quantise(qs_grouped, "qs")
-        gather_words(640, 1024)
+        gather_words(CUT_QS, CUT_QE)
         qe_mx = quantise(qe_grouped, "qe")
+        gather_words(CUT_QE, I)
 
-        def score(q_mx, name, widths):
-            table = sb.tile([P, I], F32, name=name)
-            first = 0
-            for width in widths:
-                bank = ps.tile([P, width], F32, name=name + "_bank", tag="bank", bufs=8)
+        a_sb = sb.tile([P, I], F32, name="a_sb")
+        b_sb = sb.tile([P, I], F32, name="b_sb")
+
+        def score(q_mx, table, first, last, width, empty):
+            for left in range(first, last, width):
+                bank = ps.tile([P, width], F32, name="bank", tag="bank", bufs=8)
                 nc.tensor.matmul_mx(
                     bank[:],
                     lhsT=q_mx[0][:].bitcast(FP8X4),
                     lhsT_scale=q_mx[1][:],
-                    rhs=codes_of(first, first + width).bitcast(FP8X4),
-                    rhs_scale=tok_plane[:, first : first + width],
+                    rhs=codes_of(left, left + width).bitcast(FP8X4),
+                    rhs_scale=tok_plane[:, left : left + width],
                     start=True,
                     stop=True,
                 )
-                nc.scalar.copy(table[:, first : first + width], bank[:])
-                first = first + width
-            return table
+                empty(table[:, left : left + width], bank[:])
 
-        a_sb = score(qs_mx, "a_sb", (128,) * (I // 128))
-        b_sb = score(qe_mx, "b_sb", (128,) * (I // 128))
+        score(qs_mx, a_sb, 0, 768, 256, nc.scalar.copy)
+        score(qe_mx, b_sb, 0, 256, 256, nc.scalar.copy)
+        score(qe_mx, b_sb, 256, 384, 128, nc.vector.tensor_copy)
+        score(qs_mx, a_sb, 768, 896, 128, nc.scalar.copy)
+        score(qs_mx, a_sb, 896, 1024, 128, nc.vector.tensor_copy)
+        score(qe_mx, b_sb, 384, 1024, 128, nc.scalar.copy)
 
-        a_picked = sb.tile([P, J], F32, name="a_picked")
+        def starts(first, last):
+            return a_sb[:].indirect(start_list[:, columns(first, last)])
+
+        def ends(first, last):
+            return b_sb[:].indirect(end_list[:, columns(first, last)])
+
+        a_early = sb.tile([P, VECTOR_STARTS], F32, name="a_early")
+        a_late = sb.tile([P, J - VECTOR_STARTS], F32, name="a_late", tag="stage_e", align_bytes=64)
+        b_picked = sb.tile([P, SCALAR_ENDS], F32, name="b_picked")
         s = sb.tile([P, J], F32, name="s")
-        for first in range(0, J, SPAN_PIECE):
-            last = first + SPAN_PIECE
-            nc.vector.tensor_copy(a_picked[:, first:last], a_sb[:].indirect(start_list[:, columns(first, last)]))
-        for first in range(0, J, SPAN_PIECE):
-            last = first + SPAN_PIECE
-            nc.vector.tensor_tensor(
-                s[:, first:last], b_sb[:].indirect(end_list[:, columns(first, last)]), a_picked[:, first:last], ALU.add
-            )
+        nc.vector.tensor_copy(a_early[:], starts(0, VECTOR_STARTS))
+        nc.scalar.activation(a_late[:], starts(VECTOR_STARTS, J), ACT.Copy)
+        nc.scalar.activation(b_picked[:], ends(0, SCALAR_ENDS), ACT.Copy)
+        nc.vector.tensor_tensor(
+            s[:, SCALAR_ENDS:VECTOR_STARTS], ends(SCALAR_ENDS, VECTOR_STARTS), a_early[:, SCALAR_ENDS:], ALU.add
+        )
+        nc.vector.tensor_tensor(s[:, VECTOR_STARTS:], ends(VECTOR_STARTS, J), a_late[:], ALU.add)
+        nc.vector.tensor_tensor(s[:, :SCALAR_ENDS], b_picked[:], a_early[:, :SCALAR_ENDS], ALU.add)
 
         neg_max = sb.tile([P, 1], F32, name="neg_max")
         nc.vector.tensor_reduce(neg_max[:], s[:], AXIS.X, ALU.max, negate=True)

@@ -19,11 +19,11 @@ D, T, I, J, Q = 512, 2048, 1024, 512, 128
 PER_COLUMN = 16
 QUADRANT = 32
 SCALE_ROW0 = 112
-VECTOR_STARTS = 320
+VECTOR_STARTS = 384
 SCALAR_ENDS = 128
 STORE_PIECE = 128
-CUT_QS = 512
-CUT_QE = 768
+CUT_QS = 640
+CUT_LAST = 896
 FLOPS = 2 * 2 * D * Q * I
 
 
@@ -42,7 +42,7 @@ def tile_attend_spanpointer_kernel(tc, qs, qe, tok_words, tok_scales, offs, offs
         words = sb.tile([P, T], I32, name="words", align_bytes=64)
         scales = sb.tile([P, T], U8, name="scales", align_bytes=64)
         qs_raw = sb.tile([P, PACK, Q], F32, name="qs_raw", tag="stage_s", align_bytes=64)
-        qe_raw = sb.tile([P, PACK, Q], F32, name="qe_raw", tag="stage_e", align_bytes=64)
+        qe_raw = sb.tile([P, PACK, Q], F32, name="qe_raw", align_bytes=64)
         tok_plane = sb.tile([P, I], U8, name="tok_plane", align_bytes=64)
 
         nc.vector.memset(scales[:SCALE_ROW0, :].bitcast(I32), 0)
@@ -82,15 +82,12 @@ def tile_attend_spanpointer_kernel(tc, qs, qe, tok_words, tok_scales, offs, offs
             )
 
         early_codes = sb.tile([P, CUT_QS], U32, name="early_codes", align_bytes=64)
-        middle_codes = sb.tile([P, CUT_QE - CUT_QS], U32, name="middle_codes", tag="stage_s", align_bytes=64)
-        late_codes = sb.tile([P, I - CUT_QE], U32, name="late_codes", tag="stage_e", align_bytes=64)
+        late_codes = sb.tile([P, I - CUT_QS], U32, name="late_codes", tag="stage_s", align_bytes=64)
 
         def codes_of(first, last):
             if first < CUT_QS:
                 return early_codes[:, first:last]
-            if first < CUT_QE:
-                return middle_codes[:, first - CUT_QS : last - CUT_QS]
-            return late_codes[:, first - CUT_QE : last - CUT_QE]
+            return late_codes[:, first - CUT_QS : last - CUT_QS]
 
         def gather_words(first, last):
             nc.vector.tensor_copy(
@@ -99,9 +96,9 @@ def tile_attend_spanpointer_kernel(tc, qs, qe, tok_words, tok_scales, offs, offs
 
         gather_words(0, CUT_QS)
         qs_mx = quantise(qs_grouped, "qs")
-        gather_words(CUT_QS, CUT_QE)
+        gather_words(CUT_QS, CUT_LAST)
+        gather_words(CUT_LAST, I)
         qe_mx = quantise(qe_grouped, "qe")
-        gather_words(CUT_QE, I)
 
         a_sb = sb.tile([P, I], F32, name="a_sb")
         b_sb = sb.tile([P, I], F32, name="b_sb")
@@ -120,12 +117,8 @@ def tile_attend_spanpointer_kernel(tc, qs, qe, tok_words, tok_scales, offs, offs
                 )
                 empty(table[:, left : left + width], bank[:])
 
-        score(qs_mx, a_sb, 0, 768, 256, nc.scalar.copy)
-        score(qe_mx, b_sb, 0, 256, 256, nc.scalar.copy)
-        score(qe_mx, b_sb, 256, 384, 128, nc.vector.tensor_copy)
-        score(qs_mx, a_sb, 768, 896, 128, nc.scalar.copy)
-        score(qs_mx, a_sb, 896, 1024, 128, nc.vector.tensor_copy)
-        score(qe_mx, b_sb, 384, 1024, 128, nc.scalar.copy)
+        score(qs_mx, a_sb, 0, I, 128, nc.scalar.copy)
+        score(qe_mx, b_sb, 0, I, 128, nc.scalar.copy)
 
         def starts(first, last):
             return a_sb[:].indirect(start_list[:, columns(first, last)])
@@ -134,7 +127,7 @@ def tile_attend_spanpointer_kernel(tc, qs, qe, tok_words, tok_scales, offs, offs
             return b_sb[:].indirect(end_list[:, columns(first, last)])
 
         a_early = sb.tile([P, VECTOR_STARTS], F32, name="a_early")
-        a_late = sb.tile([P, J - VECTOR_STARTS], F32, name="a_late", tag="stage_e", align_bytes=64)
+        a_late = sb.tile([P, J - VECTOR_STARTS], F32, name="a_late", tag="stage_s", align_bytes=64)
         b_picked = sb.tile([P, SCALAR_ENDS], F32, name="b_picked")
         s = sb.tile([P, J], F32, name="s")
         nc.vector.tensor_copy(a_early[:], starts(0, VECTOR_STARTS))

@@ -20,7 +20,7 @@ PER_COLUMN = 16
 QUADRANT = 32
 SCALE_ROW0 = 112
 VECTOR_STARTS = 384
-SCALAR_ENDS = 128
+SCALAR_ENDS = 192
 STORE_PIECE = 128
 CUT_QS = 640
 CUT_LAST = 896
@@ -129,21 +129,21 @@ def tile_attend_spanpointer_kernel(tc, qs, qe, tok_words, tok_scales, offs, offs
         a_early = sb.tile([P, VECTOR_STARTS], F32, name="a_early")
         a_late = sb.tile([P, J - VECTOR_STARTS], F32, name="a_late", tag="stage_s", align_bytes=64)
         b_picked = sb.tile([P, SCALAR_ENDS], F32, name="b_picked")
-        s = sb.tile([P, J], F32, name="s")
+        s = sb.tile([P, J + 1], F32, name="s")
+        head = VECTOR_STARTS - SCALAR_ENDS
         nc.vector.tensor_copy(a_early[:], starts(0, VECTOR_STARTS))
         nc.scalar.activation(a_late[:], starts(VECTOR_STARTS, J), ACT.Copy)
-        nc.scalar.activation(b_picked[:], ends(0, SCALAR_ENDS), ACT.Copy)
-        nc.vector.tensor_tensor(
-            s[:, SCALAR_ENDS:VECTOR_STARTS], ends(SCALAR_ENDS, VECTOR_STARTS), a_early[:, SCALAR_ENDS:], ALU.add
-        )
-        nc.vector.tensor_tensor(s[:, VECTOR_STARTS:], ends(VECTOR_STARTS, J), a_late[:], ALU.add)
-        nc.vector.tensor_tensor(s[:, :SCALAR_ENDS], b_picked[:], a_early[:, :SCALAR_ENDS], ALU.add)
+        nc.scalar.activation(b_picked[:], ends(head, VECTOR_STARTS), ACT.Copy)
+        nc.vector.tensor_tensor(s[:, :head], ends(0, head), a_early[:, :head], ALU.add)
+        nc.vector.tensor_tensor(s[:, VECTOR_STARTS:J], ends(VECTOR_STARTS, J), a_late[:], ALU.add)
+        nc.vector.tensor_reduce(s[:, J:], s[:, :head], AXIS.X, ALU.max)
+        nc.vector.tensor_tensor(s[:, head:VECTOR_STARTS], b_picked[:], a_early[:, head:], ALU.add)
 
         neg_max = sb.tile([P, 1], F32, name="neg_max")
-        nc.vector.tensor_reduce(neg_max[:], s[:], AXIS.X, ALU.max, negate=True)
+        nc.vector.tensor_reduce(neg_max[:], s[:, head:], AXIS.X, ALU.max, negate=True)
         p = sb.tile([P, J], F32, name="p")
         row_sum = sb.tile([P, 1], F32, name="row_sum")
-        nc.scalar.activation(p[:], s[:], ACT.Exp, bias=neg_max[:], accum_out=row_sum[:])
+        nc.scalar.activation(p[:], s[:, :J], ACT.Exp, bias=neg_max[:], accum_out=row_sum[:])
         inv_sum = sb.tile([P, 1], F32, name="inv_sum")
         nc.vector.reciprocal(inv_sum[:], row_sum[:])
         y = sb.tile([P, J], F32, name="y")

@@ -19,7 +19,7 @@ D, T, I, J, Q = 512, 2048, 1024, 512, 128
 PER_COLUMN = 16
 QUADRANT = 32
 SCALE_ROW0 = 112
-VECTOR_STARTS = 384
+SCALAR_STARTS = 160
 SCALAR_ENDS = 192
 STORE_PIECE = 128
 CUT_QS = 640
@@ -126,21 +126,24 @@ def tile_attend_spanpointer_kernel(tc, qs, qe, tok_words, tok_scales, offs, offs
         def ends(first, last):
             return b_sb[:].indirect(end_list[:, columns(first, last)])
 
-        a_early = sb.tile([P, VECTOR_STARTS], F32, name="a_early")
-        a_late = sb.tile([P, J - VECTOR_STARTS], F32, name="a_late", tag="stage_s", align_bytes=64)
+        a_late = sb.tile([P, SCALAR_STARTS], F32, name="a_late", tag="stage_s", align_bytes=64)
+        a_early = sb.tile([P, J - SCALAR_STARTS], F32, name="a_early")
         b_picked = sb.tile([P, SCALAR_ENDS], F32, name="b_picked")
-        s = sb.tile([P, J + 1], F32, name="s")
-        head = VECTOR_STARTS - SCALAR_ENDS
-        nc.vector.tensor_copy(a_early[:], starts(0, VECTOR_STARTS))
-        nc.scalar.activation(a_late[:], starts(VECTOR_STARTS, J), ACT.Copy)
-        nc.scalar.activation(b_picked[:], ends(head, VECTOR_STARTS), ACT.Copy)
-        nc.vector.tensor_tensor(s[:, :head], ends(0, head), a_early[:, :head], ALU.add)
-        nc.vector.tensor_tensor(s[:, VECTOR_STARTS:J], ends(VECTOR_STARTS, J), a_late[:], ALU.add)
-        nc.vector.tensor_reduce(s[:, J:], s[:, :head], AXIS.X, ALU.max)
-        nc.vector.tensor_tensor(s[:, head:VECTOR_STARTS], b_picked[:], a_early[:, head:], ALU.add)
+        s = sb.tile([P, J + 2], F32, name="s")
+        tail = J - SCALAR_ENDS
+        nc.vector.tensor_copy(a_early[:], starts(SCALAR_STARTS, J))
+        nc.scalar.activation(a_late[:], starts(0, SCALAR_STARTS), ACT.Copy)
+        nc.scalar.activation(b_picked[:], ends(tail, J), ACT.Copy)
+        nc.vector.tensor_tensor(
+            s[:, SCALAR_STARTS:tail], ends(SCALAR_STARTS, tail), a_early[:, : tail - SCALAR_STARTS], ALU.add
+        )
+        nc.vector.tensor_tensor(s[:, :SCALAR_STARTS], ends(0, SCALAR_STARTS), a_late[:], ALU.add)
+        nc.vector.tensor_reduce(s[:, J : J + 1], s[:, SCALAR_STARTS:tail], AXIS.X, ALU.max)
+        nc.vector.tensor_reduce(s[:, J + 1 :], s[:, :SCALAR_STARTS], AXIS.X, ALU.max)
+        nc.vector.tensor_tensor(s[:, tail:J], b_picked[:], a_early[:, tail - SCALAR_STARTS :], ALU.add)
 
         neg_max = sb.tile([P, 1], F32, name="neg_max")
-        nc.vector.tensor_reduce(neg_max[:], s[:, head:], AXIS.X, ALU.max, negate=True)
+        nc.vector.tensor_reduce(neg_max[:], s[:, tail:], AXIS.X, ALU.max, negate=True)
         p = sb.tile([P, J], F32, name="p")
         row_sum = sb.tile([P, 1], F32, name="row_sum")
         nc.scalar.activation(p[:], s[:, :J], ACT.Exp, bias=neg_max[:], accum_out=row_sum[:])

@@ -20,7 +20,7 @@ PER_COLUMN = 16
 QUADRANT = 32
 SCALE_ROW0 = 112
 SCALAR_STARTS = 160
-SCALAR_ENDS = 192
+SCALAR_ENDS = 224
 STORE_PIECE = 128
 CUT_QS = 640
 CUT_LAST = 896
@@ -129,24 +129,21 @@ def tile_attend_spanpointer_kernel(tc, qs, qe, tok_words, tok_scales, offs, offs
         a_late = sb.tile([P, SCALAR_STARTS], F32, name="a_late", tag="stage_s", align_bytes=64)
         a_early = sb.tile([P, J - SCALAR_STARTS], F32, name="a_early")
         b_picked = sb.tile([P, SCALAR_ENDS], F32, name="b_picked")
-        s = sb.tile([P, J + 2], F32, name="s")
-        tail = J - SCALAR_ENDS
+        s = sb.tile([P, J + 1], F32, name="s")
+        both = SCALAR_STARTS + SCALAR_ENDS
         nc.vector.tensor_copy(a_early[:], starts(SCALAR_STARTS, J))
         nc.scalar.activation(a_late[:], starts(0, SCALAR_STARTS), ACT.Copy)
-        nc.scalar.activation(b_picked[:], ends(tail, J), ACT.Copy)
-        nc.vector.tensor_tensor(
-            s[:, SCALAR_STARTS:tail], ends(SCALAR_STARTS, tail), a_early[:, : tail - SCALAR_STARTS], ALU.add
-        )
-        nc.vector.tensor_tensor(s[:, :SCALAR_STARTS], ends(0, SCALAR_STARTS), a_late[:], ALU.add)
-        nc.vector.tensor_reduce(s[:, J : J + 1], s[:, SCALAR_STARTS:tail], AXIS.X, ALU.max)
-        nc.vector.tensor_reduce(s[:, J + 1 :], s[:, :SCALAR_STARTS], AXIS.X, ALU.max)
-        nc.vector.tensor_tensor(s[:, tail:J], b_picked[:], a_early[:, tail - SCALAR_STARTS :], ALU.add)
+        nc.scalar.activation(b_picked[:], ends(SCALAR_STARTS, both), ACT.Copy)
+        nc.vector.tensor_tensor(s[:, 1 + both :], ends(both, J), a_early[:, SCALAR_ENDS:], ALU.add)
+        nc.vector.tensor_tensor(s[:, 1 : 1 + SCALAR_STARTS], ends(0, SCALAR_STARTS), a_late[:], ALU.add)
+        nc.vector.tensor_reduce(s[:, :1], s[:, 1 + both :], AXIS.X, ALU.max)
+        nc.vector.tensor_tensor(s[:, 1 + SCALAR_STARTS : 1 + both], b_picked[:], a_early[:, :SCALAR_ENDS], ALU.add)
 
         neg_max = sb.tile([P, 1], F32, name="neg_max")
-        nc.vector.tensor_reduce(neg_max[:], s[:, tail:], AXIS.X, ALU.max, negate=True)
+        nc.vector.tensor_reduce(neg_max[:], s[:, : 1 + both], AXIS.X, ALU.max, negate=True)
         p = sb.tile([P, J], F32, name="p")
         row_sum = sb.tile([P, 1], F32, name="row_sum")
-        nc.scalar.activation(p[:], s[:, :J], ACT.Exp, bias=neg_max[:], accum_out=row_sum[:])
+        nc.scalar.activation(p[:], s[:, 1:], ACT.Exp, bias=neg_max[:], accum_out=row_sum[:])
         inv_sum = sb.tile([P, 1], F32, name="inv_sum")
         nc.vector.reciprocal(inv_sum[:], row_sum[:])
         y = sb.tile([P, J], F32, name="y")

from contextlib import ExitStack

import concourse.mybir as mybir

F32 = mybir.dt.float32
BF16 = mybir.dt.bfloat16
I32 = mybir.dt.int32
U32 = mybir.dt.uint32
U16 = mybir.dt.uint16
U8 = mybir.dt.uint8
FP8X4 = mybir.dt.float8_e4m3fn_x4
ALU = mybir.AluOpType
ACT = mybir.ActivationFunctionType
AXIS = mybir.AxisListType

P = 128
PACK = 4
D, T, I, J, Q = 512, 2048, 1024, 512, 128
PER_COLUMN = 16
QUADRANT = 32
SCALE_ROW0 = 112
SCALAR_STARTS = 160
SCALAR_ENDS = 224
STORE_PIECE = 128
CUT_QS = 640
CUT_LAST = 896
FLOPS = 2 * 2 * D * Q * I


def tile_attend_spanpointer_kernel(tc, qs, qe, tok_words, tok_scales, offs, offs2, offs3, out):
    nc = tc.nc
    with ExitStack() as ctx:
        sb = ctx.enter_context(tc.tile_pool(name="sb", bufs=1))
        ps = ctx.enter_context(tc.psum_pool(name="ps", bufs=1))

        def columns(first, last):
            return slice(first // PER_COLUMN, last // PER_COLUMN)

        slot_list = sb.tile([P, I // PER_COLUMN], U16, name="slot_list")
        start_list = sb.tile([P, J // PER_COLUMN], U16, name="start_list")
        end_list = sb.tile([P, J // PER_COLUMN], U16, name="end_list")
        words = sb.tile([P, T], I32, name="words", align_bytes=64)
        scales = sb.tile([P, T], U8, name="scales", align_bytes=64)
        qs_raw = sb.tile([P, PACK, Q], F32, name="qs_raw", tag="stage_s", align_bytes=64)
        qe_raw = sb.tile([P, PACK, Q], F32, name="qe_raw", align_bytes=64)
        tok_plane = sb.tile([P, I], U8, name="tok_plane", align_bytes=64)

        nc.vector.memset(scales[:SCALE_ROW0, :].bitcast(I32), 0)
        nc.vector.memset(tok_plane[P - QUADRANT :, :].bitcast(I32), 0)
        nc.vector.tensor_copy(tok_plane[: P - QUADRANT, :].bitcast(I32), scales[: P - QUADRANT, :I].bitcast(I32))

        nc.scalar.dma_start(scales[SCALE_ROW0:, :].bitcast(I32), tok_scales[0].bitcast(I32))
        nc.sync.dma_start(slot_list[:], offs)
        nc.sync.dma_start(words[:], tok_words[0].rearrange("p n t -> p (n t)").bitcast(I32))
        nc.sync.dma_start(qs_raw[:], qs.rearrange("(p t) q -> p t q", t=PACK))
        nc.sync.dma_start(qe_raw[:], qe.rearrange("(p t) q -> p t q", t=PACK))
        nc.sync.dma_start(start_list[:], offs2)
        nc.sync.dma_start(end_list[:], offs3)

        def interleave(raw, name):
            grouped = sb.tile([P, Q, PACK], BF16, name=name + "_grouped", align_bytes=64)
            nc.scalar.copy(
                grouped[:].rearrange("p (c i) t -> p c t i", i=4), raw[:].rearrange("p t (c i) -> p c t i", i=4)
            )
            return grouped

        def quantise(grouped, name):
            codes = sb.tile([P, Q], U32, name=name + "_codes", align_bytes=64)
            plane = sb.tile([P, Q], U8, name=name + "_plane", align_bytes=64)
            nc.vector.quantize_mx(codes[:].bitcast(FP8X4), plane[:], grouped[:].rearrange("p q t -> p (q t)"))
            return codes, plane

        qs_grouped = interleave(qs_raw, "qs")
        qe_grouped = interleave(qe_raw, "qe")

        picked = sb.tile([P, I], U8, name="picked", align_bytes=64)
        nc.vector.tensor_copy(picked[:], scales[:].indirect(slot_list[:]))
        for quad in (0, 2, 1, 3):
            nc.sync.dma_start(
                tok_plane[QUADRANT * quad : QUADRANT * quad + PACK, :].bitcast(I32),
                picked[SCALE_ROW0 + PACK * quad : SCALE_ROW0 + PACK * (quad + 1), :].bitcast(I32),
            )

        early_codes = sb.tile([P, CUT_QS], U32, name="early_codes", align_bytes=64)
        late_codes = sb.tile([P, I - CUT_QS], U32, name="late_codes", tag="stage_s", align_bytes=64)

        def codes_of(first, last):
            if first < CUT_QS:
                return early_codes[:, first:last]
            return late_codes[:, first - CUT_QS : last - CUT_QS]

        def gather_words(first, last):
            nc.vector.tensor_copy(
                codes_of(first, last), words[:].bitcast(U32).indirect(slot_list[:, columns(first, last)])
            )

        gather_words(0, CUT_QS)
        qs_mx = quantise(qs_grouped, "qs")
        gather_words(CUT_QS, CUT_LAST)
        gather_words(CUT_LAST, I)
        qe_mx = quantise(qe_grouped, "qe")

        a_sb = sb.tile([P, I], F32, name="a_sb")
        b_sb = sb.tile([P, I], F32, name="b_sb")

        def score(q_mx, table, first, last, width, empty):
            for left in range(first, last, width):
                bank = ps.tile([P, width], F32, name="bank", tag="bank", bufs=8)
                nc.tensor.matmul_mx(
                    bank[:],
                    lhsT=q_mx[0][:].bitcast(FP8X4),
                    lhsT_scale=q_mx[1][:],
                    rhs=codes_of(left, left + width).bitcast(FP8X4),
                    rhs_scale=tok_plane[:, left : left + width],
                    start=True,
                    stop=True,
                )
                empty(table[:, left : left + width], bank[:])

        score(qs_mx, a_sb, 0, I, 128, nc.scalar.copy)
        score(qe_mx, b_sb, 0, I, 128, nc.scalar.copy)

        def starts(first, last):
            return a_sb[:].indirect(start_list[:, columns(first, last)])

        def ends(first, last):
            return b_sb[:].indirect(end_list[:, columns(first, last)])

        a_late = sb.tile([P, SCALAR_STARTS], F32, name="a_late", tag="stage_s", align_bytes=64)
        a_early = sb.tile([P, J - SCALAR_STARTS], F32, name="a_early")
        b_picked = sb.tile([P, SCALAR_ENDS], F32, name="b_picked")
        s = sb.tile([P, J + 1], F32, name="s")
        both = SCALAR_STARTS + SCALAR_ENDS
        nc.vector.tensor_copy(a_early[:], starts(SCALAR_STARTS, J))
        nc.scalar.activation(a_late[:], starts(0, SCALAR_STARTS), ACT.Copy)
        nc.scalar.activation(b_picked[:], ends(SCALAR_STARTS, both), ACT.Copy)
        nc.vector.tensor_tensor(s[:, 1 + both :], ends(both, J), a_early[:, SCALAR_ENDS:], ALU.add)
        nc.vector.tensor_tensor(s[:, 1 : 1 + SCALAR_STARTS], ends(0, SCALAR_STARTS), a_late[:], ALU.add)
        nc.vector.tensor_reduce(s[:, :1], s[:, 1 + both :], AXIS.X, ALU.max)
        nc.vector.tensor_tensor(s[:, 1 + SCALAR_STARTS : 1 + both], b_picked[:], a_early[:, :SCALAR_ENDS], ALU.add)

        neg_max = sb.tile([P, 1], F32, name="neg_max")
        nc.vector.tensor_reduce(neg_max[:], s[:, : 1 + both], AXIS.X, ALU.max, negate=True)
        p = sb.tile([P, J], F32, name="p")
        row_sum = sb.tile([P, 1], F32, name="row_sum")
        nc.scalar.activation(p[:], s[:, 1:], ACT.Exp, bias=neg_max[:], accum_out=row_sum[:])
        inv_sum = sb.tile([P, 1], F32, name="inv_sum")
        nc.vector.reciprocal(inv_sum[:], row_sum[:])
        y = sb.tile([P, J], F32, name="y")
        for v in range(J // STORE_PIECE):
            spans = slice(v * STORE_PIECE, (v + 1) * STORE_PIECE)
            nc.vector.tensor_scalar(y[:, spans], p[:, spans], inv_sum[:], float(J), ALU.mult, ALU.mult)
            (nc.sync, nc.scalar)[v % 2].dma_start(out[:, spans], y[:, spans])
